import numpy as np, ml_dtypes
CORES = [36,164,52,180,100,228,116,244]
N = 8
import mx_ref
NC, WT = 128, 2
BF = ml_dtypes.bfloat16
def pk(c, s, i=0):
    return (np.ascontiguousarray(c[:, 512 * i:512 * i + 512]), mx_ref.live(s[:, 128 * i:128 * i + 128]))
def inputs(rng, e, E):
    def f(*shape):
        v = (rng.standard_normal(shape, dtype=np.float32) * np.exp2(rng.integers(-2, 3, shape[:-1] + (1,)))).astype(BF)
        return mx_ref.spread((v.astype(np.float32) * np.exp2(rng.integers(-E, E + 1, shape[:-2] + (1, 1))).astype(np.float32)).astype(BF), rng, e)
    def packed(k):
        c = np.zeros((N, 128, k * 512), np.uint8); s = np.zeros((N, 128, k * 128), np.uint8)
        for r in range(N):
            for i in range(k):
                a, b = mx_ref.quantize(f(128, 512)); c[r][:, 512 * i:512 * i + 512] = a; s[r][:, 128 * i:128 * i + 128] = mx_ref.plane(b, rng)
        return c, s
    d = {}
    d["wc"], d["ws"] = packed(WT)
    d["x"] = f(N, 128, 4 * NC)
    return d
def setup_inputs(rng):
    return inputs(rng, 0, 0)
def setup_inputs_blocks(rng):
    return inputs(rng, 4, 0)
def setup_inputs_wide(rng):
    return inputs(rng, 0, 8)
def reference(wc, ws, x):
    y = np.zeros((N, 128, N * WT * NC), np.float32)
    for r in range(N):
        X = mx_ref.quantize(x[r])
        for b in range(N * WT):
            y[r][:, NC * b:NC * b + NC] = mx_ref.matmul(pk(wc[b // WT], ws[b // WT], b % WT), X)
    return {"y": y}

@@ -1,0 +1,128 @@
+from concourse.bass import DstId, RemoteDMATransfer
+from concourse.mybir import dt
+
+N, WT, NC = 8, 2, 128
+NT = N * WT
+SIM = 256
+NW, NY, NBANK = 3, 2, 8
+OWN = (1, 2)
+TEAM = (("far", 0, (3, 6)), ("near", 0, (4, 7)), ("far", 1, (5,)))
+ORDER = (1, 2, 3, 4, 5, 6, 7)
+
+SCRATCH = {
+    "xb": ("sbuf", [128, 4 * NC], "bfloat16"),
+    "xq": ("sbuf", [128, NC], "float8_e4m3fn_x4"),
+    "xs": ("sbuf", [128, NC], "uint8"),
+    "wq": ("sbuf", [128, NW * NC], "float8_e4m3fn_x4"),
+    "wp": ("sbuf", [128, NW * NC], "uint8"),
+    "yo": ("sbuf", [128, NY * NC], "float32"),
+    "ps": ("psum", [128, NBANK * 512], "float32"),
+    "sc": ("dram", [128, WT * NC], "float8_e4m3fn_x4"),
+    "sp": ("dram", [128, WT * NC], "uint8"),
+}
+for _o in range(1, N):
+    SCRATCH["lc%d" % _o] = ("dram", [128, WT * NC], "float8_e4m3fn_x4")
+    SCRATCH["lp%d" % _o] = ("dram", [128, WT * NC], "uint8")
+
+SEMAPHORES = (["stg", "xl", "xqd", "got", "left"] + ["arr%d" % o for o in range(1, N)]
+              + ["%s%d" % (s, t) for s in ("fw", "mm", "cp", "st") for t in range(NT)])
+
+
+def _ship(g, core, T, topo, plan, sem):
+    mask = topo.mask(core, plan[0][0])
+    for p in plan:
+        mask &= topo.mask(core, p[0])
+    k = bin(mask).count("1")
+    ids = [topo.addr(p[0], core) for p in plan]
+    for part in (0, 1):
+        src = T.sc[:].bitcast(dt.uint8) if part == 0 else T.sp[:]
+        outs = [T[p[1]][:].bitcast(dt.uint8) if part == 0 else T[p[2]][:] for p in plan]
+        if len(plan) == 1:
+            g.remote_dma(out_ap=outs[0], in_ap=src, remote_sem=sem, local_sem=T.sem.left,
+                         pid=ids[0][1], routing_id=ids[0][0], dma_engine_mask=mask)
+        else:
+            g.remote_dma_fused([RemoteDMATransfer(dst_ids=[DstId(rid=a, pnc=b) for a, b in ids], dma_engine_mask=mask,
+                                                  remote_sem=sem, srcs=[src], dsts=outs)], local_sem=T.sem.left)
+    return 2 * k, 2 * k
+
+
+def rank_program(g, core, T, topo):
+    cores = list(T.cores)
+    home = None
+    for rc in cores:
+        if topo.host(rc) == topo.host(core) and topo.chip(rc) == topo.chip(core):
+            home = rc
+    if home is None:
+        return
+    r = T.rank_of(home)
+    chip = [c for c in range(SIM) if c != home and topo.host(c) == topo.host(home) and topo.chip(c) == topo.chip(home)]
+    side = {"near": [c for c in chip if topo.die(c) == topo.die(home)],
+            "far": [c for c in chip if topo.die(c) != topo.die(home)]}
+    team = [(side[s][i], offs) for s, i, offs in TEAM]
+
+    def far_write(o):
+        return _ship(g, core, T, topo, [(cores[(r + o) % N], "lc%d" % o, "lp%d" % o)], T.sem["arr%d" % o])
+
+    if core != home:
+        for h, offs in team:
+            if h == core:
+                g.wait_ge(T.sem.got, 2 * bin(topo.mask(home, core)).count("1"))
+                left = 0
+                for o in offs:
+                    left += far_write(o)[1]
+                g.wait_ge(T.sem.left, left)
+        return
+
+    S = T.sem
+    tiles = [(0, i) for i in range(WT)] + [(o, i) for o in ORDER for i in range(WT)]
+
+    g.sync.dma_start(T.sc[:].bitcast(dt.uint8), T.wc[:]).then_inc(S.stg, 16)
+    g.scalar.dma_start(T.sp[:], T.ws[:]).then_inc(S.stg, 16)
+    g.scalar.dma_start(T.xb[:], T.x[:]).then_inc(S.xl, 16)
+
+    g.wait_ge(S.stg, 32)
+    left = far_write(OWN[0])[1]
+    if team:
+        left += _ship(g, core, T, topo, [(h, "sc", "sp") for h, _ in team], S.got)[1]
+    for o in OWN[1:]:
+        left += far_write(o)[1]
+    g.wait_ge(S.left, left)
+
+    for t, (o, i) in enumerate(tiles):
+        k = t % NW
+        if o and i == 0:
+            g.sync.wait_ge(S["arr%d" % o], 2 * bin(topo.mask(cores[(r - o) % N], core)).count("1"))
+        if t >= NW:
+            g.sync.wait_ge(S["mm%d" % (t - NW)], 1)
+        if o:
+            cs, pl = T["lc%d" % o][:, NC * i:NC * (i + 1)].bitcast(dt.uint8), T["lp%d" % o][:, NC * i:NC * (i + 1)]
+        else:
+            cs, pl = T.wc[:, 4 * NC * i:4 * NC * (i + 1)], T.ws[:, NC * i:NC * (i + 1)]
+        g.sync.dma_start(T.wq[:, NC * k:NC * (k + 1)].bitcast(dt.uint8), cs).then_inc(S["fw%d" % t], 16)
+        g.sync.dma_start(T.wp[:, NC * k:NC * (k + 1)], pl).then_inc(S["fw%d" % t], 16)
+
+    g.tensor.wait_ge(S.xqd, 1)
+    for t in range(NT):
+        k, b = t % NW, t % NBANK
+        g.tensor.wait_ge(S["fw%d" % t], 32)
+        if t >= NBANK:
+            g.tensor.wait_ge(S["cp%d" % (t - NBANK)], 1)
+        g.tensor.matmul_mx(T.ps[:, 512 * b:512 * b + NC], T.wq[:, NC * k:NC * (k + 1)], T.wp[:, NC * k:NC * (k + 1)],
+                           T.xq[:], T.xs[:], True, True).then_inc(S["mm%d" % t], 1)
+
+    g.vector.wait_ge(S.xl, 16)
+    g.vector.quantize_mx(T.xq[:], T.xs[:], T.xb[:]).then_inc(S.xqd, 1)
+    for t in range(NT):
+        k, b = t % NY, t % NBANK
+        g.vector.wait_ge(S["mm%d" % t], 1)
+        if t >= NY:
+            g.vector.wait_ge(S["st%d" % (t - NY)], 16)
+        g.vector.tensor_copy(T.yo[:, NC * k:NC * (k + 1)], T.ps[:, 512 * b:512 * b + NC]).then_inc(S["cp%d" % t], 1)
+
+    for t, (o, i) in enumerate(tiles):
+        k = t % NY
+        blk = WT * ((r - o) % N) + i
+        g.scalar.wait_ge(S["cp%d" % t], 1)
+        g.scalar.dma_start(T.y[:, NC * blk:NC * (blk + 1)], T.yo[:, NC * k:NC * (k + 1)]).then_inc(S["st%d" % t], 16)
+    for t in range(NT - NY, NT):
+        g.scalar.wait_ge(S["st%d" % t], 16)

@@ -5,8 +5,7 @@ N, WT, NC = 8, 2, 128
 NT = N * WT
 SIM = 256
 NW, NY, NBANK = 3, 2, 8
-OWN = (1, 2)
-TEAM = (("far", 0, (3, 6)), ("near", 0, (4, 7)), ("far", 1, (5,)))
+WAVES = ((1, "far", 0, (3, 5, 7)), (2, "near", 0, (4, 6)))
 ORDER = (1, 2, 3, 4, 5, 6, 7)
 
 SCRATCH = {
@@ -28,22 +27,20 @@ SEMAPHORES = (["stg", "xl", "xqd", "got", "left"] + ["arr%d" % o for o in range(
               + ["%s%d" % (s, t) for s in ("fw", "mm", "cp", "st") for t in range(NT)])
 
 
-def _ship(g, core, T, topo, plan, sem):
-    mask = topo.mask(core, plan[0][0])
-    for p in plan:
-        mask &= topo.mask(core, p[0])
-    k = bin(mask).count("1")
-    ids = [topo.addr(p[0], core) for p in plan]
+def _bits(mask):
+    return bin(mask).count("1")
+
+
+def _ship(g, core, T, topo, plan):
     for part in (0, 1):
         src = T.sc[:].bitcast(dt.uint8) if part == 0 else T.sp[:]
-        outs = [T[p[1]][:].bitcast(dt.uint8) if part == 0 else T[p[2]][:] for p in plan]
-        if len(plan) == 1:
-            g.remote_dma(out_ap=outs[0], in_ap=src, remote_sem=sem, local_sem=T.sem.left,
-                         pid=ids[0][1], routing_id=ids[0][0], dma_engine_mask=mask)
-        else:
-            g.remote_dma_fused([RemoteDMATransfer(dst_ids=[DstId(rid=a, pnc=b) for a, b in ids], dma_engine_mask=mask,
-                                                  remote_sem=sem, srcs=[src], dsts=outs)], local_sem=T.sem.left)
-    return 2 * k, 2 * k
+        trs = []
+        for d, cn, pn, sem, mask in plan:
+            rid, pid = topo.addr(d, core)
+            trs.append(RemoteDMATransfer(dst_ids=[DstId(rid=rid, pnc=pid)], dma_engine_mask=mask, remote_sem=sem, src=src,
+                                         dst=T[cn][:].bitcast(dt.uint8) if part == 0 else T[pn][:]))
+        g.remote_dma_fused(trs, local_sem=T.sem.left)
+    return 2 * sum(_bits(p[4]) for p in plan)
 
 
 def rank_program(g, core, T, topo):
@@ -58,18 +55,21 @@ def rank_program(g, core, T, topo):
     chip = [c for c in range(SIM) if c != home and topo.host(c) == topo.host(home) and topo.chip(c) == topo.chip(home)]
     side = {"near": [c for c in chip if topo.die(c) == topo.die(home)],
             "far": [c for c in chip if topo.die(c) != topo.die(home)]}
-    team = [(side[s][i], offs) for s, i, offs in TEAM]
 
-    def far_write(o):
-        return _ship(g, core, T, topo, [(cores[(r + o) % N], "lc%d" % o, "lp%d" % o)], T.sem["arr%d" % o])
+    def away(o):
+        d = cores[(r + o) % N]
+        return (d, "lc%d" % o, "lp%d" % o, T.sem["arr%d" % o], topo.mask(core, d))
+
+    def inner(h, o):
+        return topo.mask(home, h) & ~topo.mask(home, cores[(r + o) % N])
 
     if core != home:
-        for h, offs in team:
-            if h == core:
-                g.wait_ge(T.sem.got, 2 * bin(topo.mask(home, core)).count("1"))
+        for o0, s, i, offs in WAVES:
+            if side[s][i] == core:
+                g.wait_ge(T.sem.got, 2 * _bits(inner(core, o0)))
                 left = 0
                 for o in offs:
-                    left += far_write(o)[1]
+                    left += _ship(g, core, T, topo, [away(o)])
                 g.wait_ge(T.sem.left, left)
         return
 
@@ -81,17 +81,16 @@ def rank_program(g, core, T, topo):
     g.scalar.dma_start(T.xb[:], T.x[:]).then_inc(S.xl, 16)
 
     g.wait_ge(S.stg, 32)
-    left = far_write(OWN[0])[1]
-    if team:
-        left += _ship(g, core, T, topo, [(h, "sc", "sp") for h, _ in team], S.got)[1]
-    for o in OWN[1:]:
-        left += far_write(o)[1]
+    left = 0
+    for o0, s, i, offs in WAVES:
+        h = side[s][i]
+        left += _ship(g, core, T, topo, [away(o0), (h, "sc", "sp", S.got, inner(h, o0))])
     g.wait_ge(S.left, left)
 
     for t, (o, i) in enumerate(tiles):
         k = t % NW
         if o and i == 0:
-            g.sync.wait_ge(S["arr%d" % o], 2 * bin(topo.mask(cores[(r - o) % N], core)).count("1"))
+            g.sync.wait_ge(S["arr%d" % o], 2 * _bits(topo.mask(cores[(r - o) % N], core)))
         if t >= NW:
             g.sync.wait_ge(S["mm%d" % (t - NW)], 1)
         if o:

from concourse.bass import DstId, RemoteDMATransfer
from concourse.mybir import dt

N, WT, NC = 8, 2, 128
NT = N * WT
SIM = 256
NW, NY, NBANK = 3, 2, 8
WAVES = ((1, "far", 0, (3, 5, 7)), (2, "near", 0, (4, 6)))
ORDER = (1, 2, 3, 4, 5, 6, 7)

SCRATCH = {
    "xb": ("sbuf", [128, 4 * NC], "bfloat16"),
    "xq": ("sbuf", [128, NC], "float8_e4m3fn_x4"),
    "xs": ("sbuf", [128, NC], "uint8"),
    "wq": ("sbuf", [128, NW * NC], "float8_e4m3fn_x4"),
    "wp": ("sbuf", [128, NW * NC], "uint8"),
    "yo": ("sbuf", [128, NY * NC], "float32"),
    "ps": ("psum", [128, NBANK * 512], "float32"),
    "sc": ("dram", [128, WT * NC], "float8_e4m3fn_x4"),
    "sp": ("dram", [128, WT * NC], "uint8"),
}
for _o in range(1, N):
    SCRATCH["lc%d" % _o] = ("dram", [128, WT * NC], "float8_e4m3fn_x4")
    SCRATCH["lp%d" % _o] = ("dram", [128, WT * NC], "uint8")

SEMAPHORES = (["stg", "xl", "xqd", "got", "left"] + ["arr%d" % o for o in range(1, N)]
              + ["%s%d" % (s, t) for s in ("fw", "mm", "cp", "st") for t in range(NT)])


def _bits(mask):
    return bin(mask).count("1")


def _ship(g, core, T, topo, plan):
    for part in (0, 1):
        src = T.sc[:].bitcast(dt.uint8) if part == 0 else T.sp[:]
        trs = []
        for d, cn, pn, sem, mask in plan:
            rid, pid = topo.addr(d, core)
            trs.append(RemoteDMATransfer(dst_ids=[DstId(rid=rid, pnc=pid)], dma_engine_mask=mask, remote_sem=sem, src=src,
                                         dst=T[cn][:].bitcast(dt.uint8) if part == 0 else T[pn][:]))
        g.remote_dma_fused(trs, local_sem=T.sem.left)
    return 2 * sum(_bits(p[4]) for p in plan)


def rank_program(g, core, T, topo):
    cores = list(T.cores)
    home = None
    for rc in cores:
        if topo.host(rc) == topo.host(core) and topo.chip(rc) == topo.chip(core):
            home = rc
    if home is None:
        return
    r = T.rank_of(home)
    chip = [c for c in range(SIM) if c != home and topo.host(c) == topo.host(home) and topo.chip(c) == topo.chip(home)]
    side = {"near": [c for c in chip if topo.die(c) == topo.die(home)],
            "far": [c for c in chip if topo.die(c) != topo.die(home)]}

    def away(o):
        d = cores[(r + o) % N]
        return (d, "lc%d" % o, "lp%d" % o, T.sem["arr%d" % o], topo.mask(core, d))

    def inner(h, o):
        return topo.mask(home, h) & ~topo.mask(home, cores[(r + o) % N])

    if core != home:
        for o0, s, i, offs in WAVES:
            if side[s][i] == core:
                g.wait_ge(T.sem.got, 2 * _bits(inner(core, o0)))
                left = 0
                for o in offs:
                    left += _ship(g, core, T, topo, [away(o)])
                g.wait_ge(T.sem.left, left)
        return

    S = T.sem
    tiles = [(0, i) for i in range(WT)] + [(o, i) for o in ORDER for i in range(WT)]

    g.sync.dma_start(T.sc[:].bitcast(dt.uint8), T.wc[:]).then_inc(S.stg, 16)
    g.scalar.dma_start(T.sp[:], T.ws[:]).then_inc(S.stg, 16)
    g.scalar.dma_start(T.xb[:], T.x[:]).then_inc(S.xl, 16)

    g.wait_ge(S.stg, 32)
    left = 0
    for o0, s, i, offs in WAVES:
        h = side[s][i]
        left += _ship(g, core, T, topo, [away(o0), (h, "sc", "sp", S.got, inner(h, o0))])
    g.wait_ge(S.left, left)

    for t, (o, i) in enumerate(tiles):
        k = t % NW
        if o and i == 0:
            g.sync.wait_ge(S["arr%d" % o], 2 * _bits(topo.mask(cores[(r - o) % N], core)))
        if t >= NW:
            g.sync.wait_ge(S["mm%d" % (t - NW)], 1)
        if o:
            cs, pl = T["lc%d" % o][:, NC * i:NC * (i + 1)].bitcast(dt.uint8), T["lp%d" % o][:, NC * i:NC * (i + 1)]
        else:
            cs, pl = T.wc[:, 4 * NC * i:4 * NC * (i + 1)], T.ws[:, NC * i:NC * (i + 1)]
        g.sync.dma_start(T.wq[:, NC * k:NC * (k + 1)].bitcast(dt.uint8), cs).then_inc(S["fw%d" % t], 16)
        g.sync.dma_start(T.wp[:, NC * k:NC * (k + 1)], pl).then_inc(S["fw%d" % t], 16)

    g.tensor.wait_ge(S.xqd, 1)
    for t in range(NT):
        k, b = t % NW, t % NBANK
        g.tensor.wait_ge(S["fw%d" % t], 32)
        if t >= NBANK:
            g.tensor.wait_ge(S["cp%d" % (t - NBANK)], 1)
        g.tensor.matmul_mx(T.ps[:, 512 * b:512 * b + NC], T.wq[:, NC * k:NC * (k + 1)], T.wp[:, NC * k:NC * (k + 1)],
                           T.xq[:], T.xs[:], True, True).then_inc(S["mm%d" % t], 1)

    g.vector.wait_ge(S.xl, 16)
    g.vector.quantize_mx(T.xq[:], T.xs[:], T.xb[:]).then_inc(S.xqd, 1)
    for t in range(NT):
        k, b = t % NY, t % NBANK
        g.vector.wait_ge(S["mm%d" % t], 1)
        if t >= NY:
            g.vector.wait_ge(S["st%d" % (t - NY)], 16)
        g.vector.tensor_copy(T.yo[:, NC * k:NC * (k + 1)], T.ps[:, 512 * b:512 * b + NC]).then_inc(S["cp%d" % t], 1)

    for t, (o, i) in enumerate(tiles):
        k = t % NY
        blk = WT * ((r - o) % N) + i
        g.scalar.wait_ge(S["cp%d" % t], 1)
        g.scalar.dma_start(T.y[:, NC * blk:NC * (blk + 1)], T.yo[:, NC * k:NC * (k + 1)]).then_inc(S["st%d" % t], 16)
    for t in range(NT - NY, NT):
        g.scalar.wait_ge(S["st%d" % t], 16)
